import numpy as np
CORES = [0,16,32,48,64,80,96,112,128,144,160,176,192,208,224,240]
N = 16
ROOT = 5
def setup_inputs(rng):
    return {"x": rng.standard_normal((N, 128, 128), dtype=np.float32)}
def reference(x):
    y = np.full(x.shape, np.nan, x.dtype)
    y[ROOT] = x.sum(axis=0, dtype=np.float64).astype(x.dtype)
    return {"y": y}

from concourse.bass import DstId, RemoteDMATransfer

NP = 16
OWNER_CORE = 4
FOLD_MASK = 0x00FF

SCRATCH = {
    "send": ("dram", [NP, 128, 8], "float32"),
    "land": ("dram", [NP, 128, 8], "float32"),
}
SEMAPHORES = ["loaded", "sent", "arrived", "folded", "stored"]


def rank_program(g, core, T, topo):
    rank = T.rank_of(core)
    root_core = T.cores[T.root]

    if rank is not None:
        g.sync.dma_start(T.send[:], T.x[:]).then_inc(T.sem.loaded, 16)
        g.wait_ge(T.sem.loaded, 16)
        for half in range(2):
            transfers = []
            for e in range(8):
                j = (rank + 1 + 8 * half + e) % NP
                rid, pid = topo.addr(T.cores[j] + OWNER_CORE, core)
                transfers.append(RemoteDMATransfer(
                    dst_ids=[DstId(rid=rid, pnc=pid)], dma_engine_mask=1 << e, remote_sem=T.sem.arrived,
                    src=T.send[j], dst=T.land[rank]))
            g.remote_dma_fused(transfers, local_sem=T.sem.sent)
        if core == root_core:
            g.sync.wait_ge(T.sem.folded, NP * 8)
            g.sync.dma_start(T.y[:], T.land[:]).then_inc(T.sem.stored, 16)
            g.wait_ge(T.sem.stored, 16)
        g.wait_ge(T.sem.sent, 16)
        return

    if core - OWNER_CORE in T.cores:
        j = T.rank_of(core - OWNER_CORE)
        g.wait_ge(T.sem.arrived, NP)
        rid, pid = topo.addr(root_core, core)
        g.remote_dma_fused([RemoteDMATransfer(
            dst_ids=[DstId(rid=rid, pnc=pid)], dma_engine_mask=FOLD_MASK, remote_sem=T.sem.folded,
            srcs=[T.land[r] for r in range(NP)], dsts=[T.land[j]], alu_op=1)], local_sem=T.sem.sent)
        g.wait_ge(T.sem.sent, 8)
